import numpy as np, ml_dtypes
CORES = [16,17,18,19,150,151]
N = 6
WB, KB, QP = 2, 1, 128
def setup_inputs(rng):
    return {"q": rng.standard_normal((N, 128, QP), dtype=np.float32).astype(ml_dtypes.bfloat16), "k": rng.standard_normal((N, 128, KB * 128), dtype=np.float32).astype(ml_dtypes.bfloat16), "v": rng.standard_normal((N, 128, KB * 128), dtype=np.float32).astype(ml_dtypes.bfloat16)}
def setup_inputs_big(rng):
    d = setup_inputs(rng)
    for k in ("q", "k", "v"): d[k] = (d[k].astype(np.float32) * 1024.0).astype(d[k].dtype)
    return d
def setup_inputs_small(rng):
    d = setup_inputs(rng)
    for k in ("q", "k", "v"): d[k] = (d[k].astype(np.float32) * (1 / 1024.0)).astype(d[k].dtype)
    return d
def setup_inputs_apart(rng):
    d = setup_inputs(rng)
    f = (10.0 ** rng.permutation(np.linspace(-1.5, 1.5, N))).astype(np.float32).reshape(N, 1, 1)
    for k in ("q", "k", "v"): d[k] = (d[k].astype(np.float32) * f).astype(d[k].dtype)
    return d
def reference(q, k, v):
    Q, K, V = q.astype(np.float64), k.astype(np.float64), v.astype(np.float64)
    y = np.zeros((N, 128, QP))
    for r in range(N):
        for j in range(max(0, r - WB), r + 1):
            for b in range(KB):
                S = np.maximum(K[j][:, 128 * b:128 * b + 128].T @ Q[r], 0.0)
                y[r] += V[j][:, 128 * b:128 * b + 128].T @ S
    return {"y": y.astype(ml_dtypes.bfloat16 if q.dtype != np.float64 else np.float64)}

@@ -1,0 +1,151 @@
+from concourse.bass import DstId, RemoteDMATransfer
+from concourse.mybir import AluOpType
+
+WB = 2
+D = 128
+RELAY = False
+CAP_ON = 4
+CAP_OFF = 4
+
+SCRATCH = {
+    "kv": ("sbuf", [128, 2 * D], "bfloat16"),
+    "qs": ("sbuf", [128, D], "bfloat16"),
+    "land1": ("sbuf", [128, 2 * D], "bfloat16"),
+    "land2": ("sbuf", [128, 2 * D], "bfloat16"),
+    "zero": ("sbuf", [128, D], "float32"),
+    "p0": ("sbuf", [128, D], "bfloat16"),
+    "p1": ("sbuf", [128, D], "bfloat16"),
+    "p2": ("sbuf", [128, D], "bfloat16"),
+    "yb": ("sbuf", [128, D], "bfloat16"),
+    "s0": ("psum", [128, 512], "float32"),
+    "s1": ("psum", [128, 512], "float32"),
+    "s2": ("psum", [128, 512], "float32"),
+    "acc": ("psum", [128, 512], "float32"),
+}
+SEMAPHORES = ["ldkv", "ldq", "arr1", "arr2", "sent", "zs", "ss0", "ss1", "ss2", "sp0", "sp1", "sp2", "so", "sy", "st"]
+
+
+def _engines(mask):
+    return [e for e in range(mask.bit_length()) if (mask >> e) & 1]
+
+
+def _pow2(n):
+    p = 1
+    while 2 * p <= n:
+        p *= 2
+    return p
+
+
+def _same_chip(topo, a, b):
+    return topo.host(a) == topo.host(b) and topo.chip(a) == topo.chip(b)
+
+
+def _routes(cores, topo):
+    n = len(cores)
+    out = []
+    for j in range(n):
+        dsts = [r for r in range(j + 1, min(n, j + WB + 1))]
+        for r in dsts:
+            s = j
+            if RELAY and not _same_chip(topo, cores[j], cores[r]):
+                first = [x for x in dsts if _same_chip(topo, cores[x], cores[r])][0]
+                if first != r:
+                    s = first
+            out.append((j, s, r))
+    return out
+
+
+def _split(topo, core, dsts):
+    order = sorted(dsts, key=lambda d: len(_engines(topo.mask(core, d))))
+    used, out = 0, {}
+    for i, d in enumerate(order):
+        m = topo.mask(core, d)
+        free = [e for e in _engines(m) if not (used >> e) & 1]
+        peers = len([x for x in order[i:] if topo.mask(core, x) == m])
+        cap = CAP_ON if _same_chip(topo, core, d) else CAP_OFF
+        k = min(_pow2(len(free) // peers), cap)
+        out[d] = sum(1 << e for e in free[:k])
+        used |= out[d]
+    return out
+
+
+def rank_program(g, core, T, topo):
+    rank = T.rank_of(core)
+    if rank is None:
+        return
+    cores = list(T.cores)
+    te, ve, sy, sc = g.tensor, g.vector, g.sync, g.scalar
+    sem = T.sem
+    routes = _routes(cores, topo)
+
+    def masks_of(s, own):
+        ds = [r for (j, x, r) in routes if x == s and (j == s) == own]
+        m = _split(topo, cores[s], [cores[r] for r in ds])
+        return dict((r, m[cores[r]]) for r in ds)
+
+    sy.dma_start(T.kv[:, 0:D], T.k[:, :]).then_inc(sem.ldkv, 16)
+    sc.dma_start(T.kv[:, D:2 * D], T.v[:, :]).then_inc(sem.ldkv, 16)
+    sy.dma_start(T.qs[:, :], T.q[:, :]).then_inc(sem.ldq, 16)
+    ve.memset(T.zero[:, :], 0.0).then_inc(sem.zs, 1)
+
+    sent = 0
+    own = masks_of(rank, True)
+    if own:
+        g.wait_ge(sem.ldkv, 32)
+        trs = []
+        for r, m in own.items():
+            rid, pid = topo.addr(cores[r], core)
+            trs.append(RemoteDMATransfer(dst_ids=[DstId(rid=rid, pnc=pid)], dma_engine_mask=m,
+                                         remote_sem=sem["arr%d" % (r - rank)], src=T.kv[:, :], dst=T["land%d" % (r - rank)][:, :]))
+            sent += len(_engines(m))
+        g.remote_dma_fused(trs, local_sem=sem.sent)
+    passed = masks_of(rank, False)
+    for (j, s, r) in routes:
+        if s == rank and j != rank:
+            m = passed[r]
+            g.wait_ge(sem["arr%d" % (rank - j)], len(_engines(masks_of(j, True)[rank])))
+            rid, pid = topo.addr(cores[r], core)
+            g.remote_dma(T["land%d" % (r - j)][:, :], T["land%d" % (rank - j)][:, :], sem["arr%d" % (r - j)], sem.sent, pid, rid, m)
+            sent += len(_engines(m))
+
+    def late(route):
+        j, s, r = route
+        off = len([1 for (a, b, c) in routes if b == s and not _same_chip(topo, cores[b], cores[c])])
+        return (s != j, not _same_chip(topo, cores[s], core), off, j)
+    inb = sorted([x for x in routes if x[2] == rank], key=late)
+    blocks = [(T.kv, None, 0)]
+    for (j, s, r) in inb:
+        blocks.append((T["land%d" % (rank - j)], sem["arr%d" % (rank - j)], len(_engines(masks_of(s, s == j)[rank]))))
+    nb = len(blocks)
+
+    def s_mm(i):
+        buf, arr, cnt = blocks[i]
+        if arr is not None:
+            te.wait_ge(arr, cnt)
+        te.matmul(T["s%d" % i][:, 0:D], buf[:, 0:D], T.qs[:, :], True, True).then_inc(sem["ss%d" % i], 1)
+
+    def o_mm(i):
+        te.wait_ge(sem["sp%d" % i], 1)
+        te.matmul(T.acc[:, 0:D], blocks[i][0][:, D:2 * D], T["p%d" % i][:, :], i == 0, i == nb - 1).then_inc(sem.so, 1)
+
+    te.wait_ge(sem.ldkv, 32)
+    te.wait_ge(sem.ldq, 16)
+    s_mm(0)
+    o_mm(0)
+    for i in range(1, nb):
+        s_mm(i)
+    for i in range(1, nb):
+        o_mm(i)
+
+    ve.wait_ge(sem.zs, 1)
+    for i in range(nb):
+        ve.wait_ge(sem["ss%d" % i], 1)
+        ve.tensor_tensor(T["p%d" % i][:, :], T["s%d" % i][:, 0:D], T.zero[:, :], AluOpType.max).then_inc(sem["sp%d" % i], 1)
+    ve.wait_ge(sem.so, nb)
+    ve.tensor_copy(T.yb[:, :], T.acc[:, 0:D]).then_inc(sem.sy, 1)
+
+    sy.wait_ge(sem.sy, 1)
+    sy.dma_start(T.y[:, :], T.yb[:, :]).then_inc(sem.st, 16)
+    sy.wait_ge(sem.st, 16)
+    if sent:
+        g.wait_ge(sem.sent, sent)

@@ -3,9 +3,8 @@ from concourse.mybir import AluOpType
 
 WB = 2
 D = 128
-RELAY = False
-CAP_ON = 4
-CAP_OFF = 4
+H = D // 2
+ENG = 8
 
 SCRATCH = {
     "kv": ("sbuf", [128, 2 * D], "bfloat16"),
@@ -18,11 +17,15 @@ SCRATCH = {
     "p2": ("sbuf", [128, D], "bfloat16"),
     "yb": ("sbuf", [128, D], "bfloat16"),
     "s0": ("psum", [128, 512], "float32"),
-    "s1": ("psum", [128, 512], "float32"),
-    "s2": ("psum", [128, 512], "float32"),
-    "acc": ("psum", [128, 512], "float32"),
+    "s1a": ("psum", [128, 512], "float32"),
+    "s1b": ("psum", [128, 512], "float32"),
+    "s2a": ("psum", [128, 512], "float32"),
+    "s2b": ("psum", [128, 512], "float32"),
+    "acca": ("psum", [128, 512], "float32"),
+    "accb": ("psum", [128, 512], "float32"),
 }
-SEMAPHORES = ["ldkv", "ldq", "arr1", "arr2", "sent", "zs", "ss0", "ss1", "ss2", "sp0", "sp1", "sp2", "so", "sy", "st"]
+SEMAPHORES = ["ldk", "ldv", "ldq", "ak1", "ak2", "av1", "av2", "sent", "zs", "ss0", "sp0",
+              "ss1a", "ss1b", "ss2a", "ss2b", "sp1a", "sp1b", "sp2a", "sp2b", "soa", "sob", "sy", "st"]
 
 
 def _engines(mask):
@@ -36,37 +39,25 @@ def _pow2(n):
     return p
 
 
-def _same_chip(topo, a, b):
-    return topo.host(a) == topo.host(b) and topo.chip(a) == topo.chip(b)
-
-
-def _routes(cores, topo):
+def _plan(cores, topo):
     n = len(cores)
-    out = []
+    calls, mask, when = {}, {}, {}
     for j in range(n):
         dsts = [r for r in range(j + 1, min(n, j + WB + 1))]
+        calls[j], mask[j] = [], 0
+        if not dsts:
+            continue
+        pool = -1
         for r in dsts:
-            s = j
-            if RELAY and not _same_chip(topo, cores[j], cores[r]):
-                first = [x for x in dsts if _same_chip(topo, cores[x], cores[r])][0]
-                if first != r:
-                    s = first
-            out.append((j, s, r))
-    return out
-
-
-def _split(topo, core, dsts):
-    order = sorted(dsts, key=lambda d: len(_engines(topo.mask(core, d))))
-    used, out = 0, {}
-    for i, d in enumerate(order):
-        m = topo.mask(core, d)
-        free = [e for e in _engines(m) if not (used >> e) & 1]
-        peers = len([x for x in order[i:] if topo.mask(core, x) == m])
-        cap = CAP_ON if _same_chip(topo, core, d) else CAP_OFF
-        k = min(_pow2(len(free) // peers), cap)
-        out[d] = sum(1 << e for e in free[:k])
-        used |= out[d]
-    return out
+            pool &= topo.mask(cores[j], cores[r])
+        pool = _engines(pool)
+        mask[j] = sum(1 << e for e in pool[:min(ENG, _pow2(len(pool)))])
+        far = dsts[-1]
+        calls[j] = [("k", far)] + [("kv", r) for r in dsts[:-1]] + [("v", far)]
+        for i, (part, r) in enumerate(calls[j]):
+            a, b = when.get((j, r), (None, None))
+            when[(j, r)] = (i if "k" in part else a, i if "v" in part else b)
+    return calls, mask, when
 
 
 def rank_program(g, core, T, topo):
@@ -76,75 +67,68 @@ def rank_program(g, core, T, topo):
     cores = list(T.cores)
     te, ve, sy, sc = g.tensor, g.vector, g.sync, g.scalar
     sem = T.sem
-    routes = _routes(cores, topo)
+    calls, mask, when = _plan(cores, topo)
 
-    def masks_of(s, own):
-        ds = [r for (j, x, r) in routes if x == s and (j == s) == own]
-        m = _split(topo, cores[s], [cores[r] for r in ds])
-        return dict((r, m[cores[r]]) for r in ds)
-
-    sy.dma_start(T.kv[:, 0:D], T.k[:, :]).then_inc(sem.ldkv, 16)
-    sc.dma_start(T.kv[:, D:2 * D], T.v[:, :]).then_inc(sem.ldkv, 16)
+    sy.dma_start(T.kv[:, 0:D], T.k[:, :]).then_inc(sem.ldk, 16)
+    sc.dma_start(T.kv[:, D:2 * D], T.v[:, :]).then_inc(sem.ldv, 16)
     sy.dma_start(T.qs[:, :], T.q[:, :]).then_inc(sem.ldq, 16)
     ve.memset(T.zero[:, :], 0.0).then_inc(sem.zs, 1)
 
     sent = 0
-    own = masks_of(rank, True)
-    if own:
-        g.wait_ge(sem.ldkv, 32)
-        trs = []
-        for r, m in own.items():
-            rid, pid = topo.addr(cores[r], core)
-            trs.append(RemoteDMATransfer(dst_ids=[DstId(rid=rid, pnc=pid)], dma_engine_mask=m,
-                                         remote_sem=sem["arr%d" % (r - rank)], src=T.kv[:, :], dst=T["land%d" % (r - rank)][:, :]))
-            sent += len(_engines(m))
-        g.remote_dma_fused(trs, local_sem=sem.sent)
-    passed = masks_of(rank, False)
-    for (j, s, r) in routes:
-        if s == rank and j != rank:
-            m = passed[r]
-            g.wait_ge(sem["arr%d" % (rank - j)], len(_engines(masks_of(j, True)[rank])))
-            rid, pid = topo.addr(cores[r], core)
-            g.remote_dma(T["land%d" % (r - j)][:, :], T["land%d" % (rank - j)][:, :], sem["arr%d" % (r - j)], sem.sent, pid, rid, m)
-            sent += len(_engines(m))
+    for (part, r) in calls[rank]:
+        c0, c1 = (D if part == "v" else 0), (D if part == "k" else 2 * D)
+        if "k" in part:
+            g.wait_ge(sem.ldk, 16)
+        if "v" in part:
+            g.wait_ge(sem.ldv, 16)
+        rid, pid = topo.addr(cores[r], core)
+        g.remote_dma(T["land%d" % (r - rank)][:, c0:c1], T.kv[:, c0:c1], sem["a%s%d" % (part[0], r - rank)], sem.sent,
+                     pid, rid, mask[rank])
+        sent += len(_engines(mask[rank]))
 
-    def late(route):
-        j, s, r = route
-        off = len([1 for (a, b, c) in routes if b == s and not _same_chip(topo, cores[b], cores[c])])
-        return (s != j, not _same_chip(topo, cores[s], core), off, j)
-    inb = sorted([x for x in routes if x[2] == rank], key=late)
-    blocks = [(T.kv, None, 0)]
-    for (j, s, r) in inb:
-        blocks.append((T["land%d" % (rank - j)], sem["arr%d" % (rank - j)], len(_engines(masks_of(s, s == j)[rank]))))
-    nb = len(blocks)
+    inb = [j for j in range(max(0, rank - WB), rank)]
+    order_s = sorted(inb, key=lambda j: (when[(j, rank)][0], -j))
+    idx = dict((j, i + 1) for i, j in enumerate(order_s))
+    events = sorted([(when[(j, rank)][0], 0, -j, j) for j in inb] + [(when[(j, rank)][1], 1, -j, j) for j in inb])
+    nb = 1 + len(inb)
+    halves = (("a", 0), ("b", H))
 
-    def s_mm(i):
-        buf, arr, cnt = blocks[i]
-        if arr is not None:
-            te.wait_ge(arr, cnt)
-        te.matmul(T["s%d" % i][:, 0:D], buf[:, 0:D], T.qs[:, :], True, True).then_inc(sem["ss%d" % i], 1)
-
-    def o_mm(i):
-        te.wait_ge(sem["sp%d" % i], 1)
-        te.matmul(T.acc[:, 0:D], blocks[i][0][:, D:2 * D], T["p%d" % i][:, :], i == 0, i == nb - 1).then_inc(sem.so, 1)
-
-    te.wait_ge(sem.ldkv, 32)
+    te.wait_ge(sem.ldk, 16)
     te.wait_ge(sem.ldq, 16)
-    s_mm(0)
-    o_mm(0)
-    for i in range(1, nb):
-        s_mm(i)
-    for i in range(1, nb):
-        o_mm(i)
+    te.matmul(T.s0[:, 0:D], T.kv[:, 0:D], T.qs[:, :], True, True).then_inc(sem.ss0, 1)
+    te.wait_ge(sem.ldv, 16)
+    te.wait_ge(sem.sp0, 1)
+    for (h, c) in halves:
+        te.matmul(T["acc" + h][:, 0:H], T.kv[:, D:2 * D], T.p0[:, c:c + H], True, nb == 1).then_inc(sem["so" + h], 1)
+    done = 1
+    for (t, kind, x, j) in events:
+        d, i, cnt = rank - j, idx[j], len(_engines(mask[j]))
+        buf = T["land%d" % d]
+        if kind == 0:
+            te.wait_ge(sem["ak%d" % d], cnt)
+            for (h, c) in halves:
+                te.matmul(T["s%d%s" % (i, h)][:, 0:H], buf[:, 0:D], T.qs[:, c:c + H], True, True).then_inc(sem["ss%d%s" % (i, h)], 1)
+        else:
+            if when[(j, rank)][0] != when[(j, rank)][1]:
+                te.wait_ge(sem["av%d" % d], cnt)
+            done += 1
+            for (h, c) in halves:
+                te.wait_ge(sem["sp%d%s" % (i, h)], 1)
+                te.matmul(T["acc" + h][:, 0:H], buf[:, D:2 * D], T["p%d" % i][:, c:c + H], False, done == nb).then_inc(sem["so" + h], 1)
 
     ve.wait_ge(sem.zs, 1)
-    for i in range(nb):
-        ve.wait_ge(sem["ss%d" % i], 1)
-        ve.tensor_tensor(T["p%d" % i][:, :], T["s%d" % i][:, 0:D], T.zero[:, :], AluOpType.max).then_inc(sem["sp%d" % i], 1)
-    ve.wait_ge(sem.so, nb)
-    ve.tensor_copy(T.yb[:, :], T.acc[:, 0:D]).then_inc(sem.sy, 1)
+    ve.wait_ge(sem.ss0, 1)
+    ve.tensor_tensor(T.p0[:, :], T.s0[:, 0:D], T.zero[:, :], AluOpType.max).then_inc(sem.sp0, 1)
+    for i in range(1, nb):
+        for (h, c) in halves:
+            ve.wait_ge(sem["ss%d%s" % (i, h)], 1)
+            ve.tensor_tensor(T["p%d" % i][:, c:c + H], T["s%d%s" % (i, h)][:, 0:H], T.zero[:, 0:H],
+                             AluOpType.max).then_inc(sem["sp%d%s" % (i, h)], 1)
+    for (h, c) in halves:
+        ve.wait_ge(sem["so" + h], nb)
+        ve.tensor_copy(T.yb[:, c:c + H], T["acc" + h][:, 0:H]).then_inc(sem.sy, 1)
 
-    sy.wait_ge(sem.sy, 1)
+    sy.wait_ge(sem.sy, 2)
     sy.dma_start(T.y[:, :], T.yb[:, :]).then_inc(sem.st, 16)
     sy.wait_ge(sem.st, 16)
     if sent:

from concourse.bass import DstId, RemoteDMATransfer
from concourse.mybir import AluOpType

WB = 2
D = 128
H = D // 2
ENG = 8

SCRATCH = {
    "kv": ("sbuf", [128, 2 * D], "bfloat16"),
    "qs": ("sbuf", [128, D], "bfloat16"),
    "land1": ("sbuf", [128, 2 * D], "bfloat16"),
    "land2": ("sbuf", [128, 2 * D], "bfloat16"),
    "zero": ("sbuf", [128, D], "float32"),
    "p0": ("sbuf", [128, D], "bfloat16"),
    "p1": ("sbuf", [128, D], "bfloat16"),
    "p2": ("sbuf", [128, D], "bfloat16"),
    "yb": ("sbuf", [128, D], "bfloat16"),
    "s0": ("psum", [128, 512], "float32"),
    "s1a": ("psum", [128, 512], "float32"),
    "s1b": ("psum", [128, 512], "float32"),
    "s2a": ("psum", [128, 512], "float32"),
    "s2b": ("psum", [128, 512], "float32"),
    "acca": ("psum", [128, 512], "float32"),
    "accb": ("psum", [128, 512], "float32"),
}
SEMAPHORES = ["ldk", "ldv", "ldq", "ak1", "ak2", "av1", "av2", "sent", "zs", "ss0", "sp0",
              "ss1a", "ss1b", "ss2a", "ss2b", "sp1a", "sp1b", "sp2a", "sp2b", "soa", "sob", "sy", "st"]


def _engines(mask):
    return [e for e in range(mask.bit_length()) if (mask >> e) & 1]


def _pow2(n):
    p = 1
    while 2 * p <= n:
        p *= 2
    return p


def _plan(cores, topo):
    n = len(cores)
    calls, mask, when = {}, {}, {}
    for j in range(n):
        dsts = [r for r in range(j + 1, min(n, j + WB + 1))]
        calls[j], mask[j] = [], 0
        if not dsts:
            continue
        pool = -1
        for r in dsts:
            pool &= topo.mask(cores[j], cores[r])
        pool = _engines(pool)
        mask[j] = sum(1 << e for e in pool[:min(ENG, _pow2(len(pool)))])
        far = dsts[-1]
        calls[j] = [("k", far)] + [("kv", r) for r in dsts[:-1]] + [("v", far)]
        for i, (part, r) in enumerate(calls[j]):
            a, b = when.get((j, r), (None, None))
            when[(j, r)] = (i if "k" in part else a, i if "v" in part else b)
    return calls, mask, when


def rank_program(g, core, T, topo):
    rank = T.rank_of(core)
    if rank is None:
        return
    cores = list(T.cores)
    te, ve, sy, sc = g.tensor, g.vector, g.sync, g.scalar
    sem = T.sem
    calls, mask, when = _plan(cores, topo)

    sy.dma_start(T.kv[:, 0:D], T.k[:, :]).then_inc(sem.ldk, 16)
    sc.dma_start(T.kv[:, D:2 * D], T.v[:, :]).then_inc(sem.ldv, 16)
    sy.dma_start(T.qs[:, :], T.q[:, :]).then_inc(sem.ldq, 16)
    ve.memset(T.zero[:, :], 0.0).then_inc(sem.zs, 1)

    sent = 0
    for (part, r) in calls[rank]:
        c0, c1 = (D if part == "v" else 0), (D if part == "k" else 2 * D)
        if "k" in part:
            g.wait_ge(sem.ldk, 16)
        if "v" in part:
            g.wait_ge(sem.ldv, 16)
        rid, pid = topo.addr(cores[r], core)
        g.remote_dma(T["land%d" % (r - rank)][:, c0:c1], T.kv[:, c0:c1], sem["a%s%d" % (part[0], r - rank)], sem.sent,
                     pid, rid, mask[rank])
        sent += len(_engines(mask[rank]))

    inb = [j for j in range(max(0, rank - WB), rank)]
    order_s = sorted(inb, key=lambda j: (when[(j, rank)][0], -j))
    idx = dict((j, i + 1) for i, j in enumerate(order_s))
    events = sorted([(when[(j, rank)][0], 0, -j, j) for j in inb] + [(when[(j, rank)][1], 1, -j, j) for j in inb])
    nb = 1 + len(inb)
    halves = (("a", 0), ("b", H))

    te.wait_ge(sem.ldk, 16)
    te.wait_ge(sem.ldq, 16)
    te.matmul(T.s0[:, 0:D], T.kv[:, 0:D], T.qs[:, :], True, True).then_inc(sem.ss0, 1)
    te.wait_ge(sem.ldv, 16)
    te.wait_ge(sem.sp0, 1)
    for (h, c) in halves:
        te.matmul(T["acc" + h][:, 0:H], T.kv[:, D:2 * D], T.p0[:, c:c + H], True, nb == 1).then_inc(sem["so" + h], 1)
    done = 1
    for (t, kind, x, j) in events:
        d, i, cnt = rank - j, idx[j], len(_engines(mask[j]))
        buf = T["land%d" % d]
        if kind == 0:
            te.wait_ge(sem["ak%d" % d], cnt)
            for (h, c) in halves:
                te.matmul(T["s%d%s" % (i, h)][:, 0:H], buf[:, 0:D], T.qs[:, c:c + H], True, True).then_inc(sem["ss%d%s" % (i, h)], 1)
        else:
            if when[(j, rank)][0] != when[(j, rank)][1]:
                te.wait_ge(sem["av%d" % d], cnt)
            done += 1
            for (h, c) in halves:
                te.wait_ge(sem["sp%d%s" % (i, h)], 1)
                te.matmul(T["acc" + h][:, 0:H], buf[:, D:2 * D], T["p%d" % i][:, c:c + H], False, done == nb).then_inc(sem["so" + h], 1)

    ve.wait_ge(sem.zs, 1)
    ve.wait_ge(sem.ss0, 1)
    ve.tensor_tensor(T.p0[:, :], T.s0[:, 0:D], T.zero[:, :], AluOpType.max).then_inc(sem.sp0, 1)
    for i in range(1, nb):
        for (h, c) in halves:
            ve.wait_ge(sem["ss%d%s" % (i, h)], 1)
            ve.tensor_tensor(T["p%d" % i][:, c:c + H], T["s%d%s" % (i, h)][:, 0:H], T.zero[:, 0:H],
                             AluOpType.max).then_inc(sem["sp%d%s" % (i, h)], 1)
    for (h, c) in halves:
        ve.wait_ge(sem["so" + h], nb)
        ve.tensor_copy(T.yb[:, c:c + H], T["acc" + h][:, 0:H]).then_inc(sem.sy, 1)

    sy.wait_ge(sem.sy, 2)
    sy.dma_start(T.y[:, :], T.yb[:, :]).then_inc(sem.st, 16)
    sy.wait_ge(sem.st, 16)
    if sent:
        g.wait_ge(sem.sent, sent)
